import numpy as np
import ml_dtypes


def mxq(x, axis, fmt="e4m3"):
    dtype, down = {"e4m3": (ml_dtypes.float8_e4m3fn, 7), "e5m2": (ml_dtypes.float8_e5m2, 14)}[fmt]
    v = np.moveaxis(np.asarray(x, np.float32).astype(ml_dtypes.bfloat16).astype(np.float64), axis, -1)
    blocks = v.reshape(v.shape[:-1] + (-1, 32))
    amax = np.abs(blocks).max(-1, keepdims=True)
    byte = np.maximum(np.where(amax > 0, np.frexp(amax)[1] - 1 + 127, 0) - down, 1)
    scale = np.exp2(byte - 127.0)
    codes = (blocks / scale).astype(np.float32).astype(dtype).astype(np.float64)
    return np.moveaxis((codes * scale).reshape(v.shape), -1, axis)


WIDE = False


def mx_kscale(k):
    if not WIDE:
        return np.ones(k)
    levels = np.array([10, -10, 5, -5, 0])
    if k % 512:
        return np.exp2(np.random.permutation(np.resize(levels, k // 32))).repeat(32)
    a = np.empty((k // 512, 16))
    for p in range(k // 512):
        a[p, :8] = np.random.permutation(np.resize(levels, 8))
        for g in range(8):
            far = levels[np.abs(levels - a[p, g]) >= 10]
            a[p, g + 8] = far[np.random.randint(len(far))]
    return np.exp2(a.ravel()).repeat(32)


def f64(x):
    return np.asarray(x).astype(np.float64)


def striped8(idx):
    return np.concatenate([v.reshape(-1, 16).T for v in idx]).astype(np.uint16)


def unstriped8(offs):
    return np.stack([offs[16 * g:16 * g + 16].T.reshape(-1) for g in range(8)]).astype(np.int64)


E2M1 = np.array([0.0, 0.5, 1.0, 1.5, 2.0, 3.0, 4.0, 6.0, -0.0, -0.5, -1.0, -1.5, -2.0, -3.0, -4.0, -6.0])


def pack_weight(w, fmt):
    k, n = w.shape
    w = f64(np.asarray(w, np.float32).astype(ml_dtypes.bfloat16)).reshape(k // 32, 32, n)
    amax = np.abs(w).max(1)
    if fmt == "e4m3":
        byte = np.frexp(amax)[1] - 1 + 127 - 7
    else:
        mant, ex = np.frexp(amax / 6.0)
        byte = np.where(mant > 0.5, ex, ex - 1) + 127
    byte = np.clip(np.where(amax > 0, byte, 1), 1, 254)
    scaled = (w * np.exp2(127.0 - byte)[:, None, :]).reshape(k, n).astype(np.float32)
    by_word = np.ascontiguousarray(scaled.reshape(k // 512, 128, 4, n).transpose(0, 1, 3, 2))
    if fmt == "e4m3":
        words = by_word.astype(ml_dtypes.float8_e4m3fn).view(np.uint8)
    else:
        c = by_word.astype(ml_dtypes.float4_e2m1fn).view(np.uint8) & 0xF
        words = (c[..., 0::2] | (c[..., 1::2] << 4)).reshape(k // 512, 128, 2 * n)
    return np.ascontiguousarray(words), np.ascontiguousarray(byte.astype(np.uint8).reshape(k // 512, 16, n))


def unpack_weight(words, scales, fmt):
    g, _, n = scales.shape
    words = np.ascontiguousarray(words).reshape(g, 128, n, -1)
    if fmt == "e4m3":
        vals = words.view(ml_dtypes.float8_e4m3fn).astype(np.float64)
    else:
        nib = np.empty((g, 128, n, 4), np.uint8)
        nib[..., 0::2] = words & 0xF
        nib[..., 1::2] = words >> 4
        vals = E2M1[nib]
    vals = vals * np.repeat(np.exp2(scales.astype(np.float64) - 127.0), 8, axis=1)[..., None]
    return vals.transpose(0, 1, 3, 2).reshape(g * 512, n)


def silu(v):
    return v / (1.0 + np.exp(-np.maximum(v, -700.0)))


K, L, M, T, S = 1024, 1024, 128, 2048, 512


def setup_inputs():
    n = np.random.standard_normal
    s1 = mx_kscale(K)[:, None]
    s2 = mx_kscale(L)[:, None]
    p_w4 = pack_weight(n((K, M)) / np.sqrt(K) / s1, "e2m1")
    return {
        "xT": (n((K, T)) * s1).astype(np.float32),
        "w4_words": p_w4[0],
        "w4_scales": p_w4[1],
        "c": (n((L, S)) * s2).astype(np.float32),
        "u": (n((L, M)) / np.sqrt(L) / s2).astype(np.float32),
        "wgt": np.repeat(np.random.uniform(0.5, 2.0, (8, S)), 16, axis=0).astype(np.float32),
        "b": (0.3 * n(128)).astype(np.float32),
        "offs": striped8(np.stack([np.random.permutation(T)[:S] for _ in range(8)])),
    }


def reference(xT, w4_words, w4_scales, c, u, wgt, b, offs):
    idx = unstriped8(offs)
    group = np.arange(K) % 512 // 64
    xg = f64(wgt)[np.arange(K) // 4 % 128] * f64(xT)[np.arange(K)[:, None], idx[group]]
    xT_ = mxq(xg, 0, "e4m3")
    w4_ = unpack_weight(w4_words, w4_scales, "e2m1")
    c_ = mxq(f64(c), 0, "e4m3")
    u_ = mxq(f64(u), 0, "e4m3")
    y = w4_.T @ xT_ + u_.T @ c_
    return silu(y + f64(b)[:, None])

@@ -1,0 +1,177 @@
+from contextlib import ExitStack
+
+import concourse.mybir as mybir
+
+K, L, M, T, S = 1024, 1024, 128, 2048, 512
+
+F32 = mybir.dt.float32
+BF16 = mybir.dt.bfloat16
+I32 = mybir.dt.int32
+U32 = mybir.dt.uint32
+U16 = mybir.dt.uint16
+U8 = mybir.dt.uint8
+E4M3X4 = mybir.dt.float8_e4m3fn_x4
+E2M1X4 = mybir.dt.float4_e2m1fn_x4
+MULT = mybir.AluOpType.mult
+SILU = mybir.ActivationFunctionType.Silu
+
+FLOPS = 2 * M * S * (K + L)
+
+P = 128
+PACK = 4
+PASSES = 2
+N_TILE = 128
+TILES = S // N_TILE
+PIECE = 256
+X_SCALAR = [512, 192]
+C_LOADS = [[(0, S)], [(0, 384), (384, S)]]
+C_SCALAR = {512: 224, 384: 128, 128: 0}
+C_QUANTIZES = {512: [(0, 512)], 384: [(0, 128), (128, 384)], 128: [(0, 128)]}
+
+
+def tile_list_hmix_silu_kernel(tc, xT, w4_words, w4_scales, c, u, wgt, b, offs, out):
+    nc = tc.nc
+    with ExitStack() as ctx:
+        lists = ctx.enter_context(tc.tile_pool(name="lists", bufs=1))
+        keep = ctx.enter_context(tc.tile_pool(name="keep", bufs=1))
+        psum = ctx.enter_context(tc.psum_pool(name="psum", bufs=1))
+
+        w4_s = keep.tile([P, PASSES * M], U8, name="w4_s", align_bytes=64)
+        w4_s_words = w4_s[:].bitcast(I32)
+        nc.vector.memset(w4_s_words, 0)
+
+        offsets = lists.tile([P, S // 16], U16, name="offsets")
+        nc.sync.dma_start(offsets[:], offs)
+        weight = keep.tile([P, S], F32, name="weight")
+        nc.sync.dma_start(weight[:], wgt)
+
+        bias = keep.tile([P, 1], F32, name="bias")
+        nc.scalar.dma_start(bias[:], b.rearrange("(p o) -> p o", o=1))
+        scales_src = w4_scales.bitcast(I32).rearrange("a q n -> q a n")
+        for q in range(4):
+            nc.scalar.dma_start(
+                w4_s_words[32 * q : 32 * q + 4, :].rearrange("p (a n) -> p a n", a=PASSES),
+                scales_src[4 * q : 4 * q + 4, :, :],
+            )
+
+        warm = keep.tile([P, 1], F32, name="warm")
+        warm_out = keep.tile([P, 1], F32, name="warm_out")
+        nc.vector.memset(warm[:], 0.0)
+        nc.scalar.activation(warm_out[:], warm[:], SILU)
+
+        x_src = xT.rearrange("(a p i) t -> a i p t", a=PASSES, i=PACK)
+        c_src = c.rearrange("(a p i) j -> a p i j", a=PASSES, i=PACK)
+        acc = [psum.tile([P, N_TILE], F32, name=f"acc{j}") for j in range(TILES)]
+        x_t = {}
+
+        def load_x(a, i):
+            x_t[a, i] = keep.tile([P, T], F32, name=f"x{a}{i}")
+            nc.sync.dma_start(x_t[a, i][:], x_src[a, i])
+
+        def gather(a, i, dst):
+            for j in range(0, S, PIECE):
+                nc.vector.tensor_tensor(
+                    dst[:, j : j + PIECE],
+                    x_t[a, i][:].indirect(offsets[:, j // 16 : (j + PIECE) // 16]),
+                    weight[:, j : j + PIECE],
+                    MULT,
+                )
+
+        def interleave(copy, grouped, rows):
+            copy(
+                grouped.rearrange("p (w v) i -> p w i v", v=4),
+                rows.rearrange("p i (w v) -> p w i v", v=4),
+            )
+
+        def share(grouped, rows, split):
+            width = rows.shape[2]
+            if split > 0:
+                interleave(nc.scalar.copy, grouped[:, 0:split, :], rows[:, :, 0:split])
+            if split < width:
+                interleave(nc.vector.tensor_copy, grouped[:, split:width, :], rows[:, :, split:width])
+
+        def quantize(codes, scales, grouped):
+            nc.vector.quantize_mx(
+                out=codes.bitcast(E4M3X4),
+                scales=scales,
+                in_=grouped.rearrange("p w i -> p (w i)"),
+            )
+
+        def operand(width, name):
+            grouped = keep.tile([P, width, PACK], BF16, name=name + "_grouped", align_bytes=64)
+            codes = keep.tile([P, width], U32, name=name + "_codes", align_bytes=64)
+            scales = keep.tile([P, width], U8, name=name + "_scales", align_bytes=64)
+            return grouped, codes, scales
+
+        def multiply(lhsT, lhsT_scale, rhs, j, start, stop):
+            cols = slice(j * N_TILE, (j + 1) * N_TILE)
+            nc.tensor.matmul_mx(
+                out=acc[j][:],
+                lhsT=lhsT,
+                lhsT_scale=lhsT_scale,
+                rhs=rhs[1][:, cols].bitcast(E4M3X4),
+                rhs_scale=rhs[2][:, cols],
+                start=start,
+                stop=stop,
+            )
+
+        for i in range(PACK):
+            load_x(0, i)
+        w4 = keep.tile([P, PASSES, 2 * M], U8, name="w4", align_bytes=64)
+        nc.sync.dma_start(w4[:], w4_words.rearrange("a p n -> p a n"))
+        u_raw = keep.tile([P, PASSES, PACK * M], F32, name="u_raw")
+        nc.sync.dma_start(u_raw[:], u.rearrange("(a p i) n -> p a (i n)", a=PASSES, i=PACK))
+        for i in range(PACK):
+            load_x(1, i)
+        c_raw = [[], []]
+        for a in range(PASSES):
+            for lo, hi in C_LOADS[a]:
+                part = keep.tile([P, PACK, hi - lo], F32, name=f"c_raw{a}_{lo}")
+                nc.sync.dma_start(part[:], c_src[a][:, :, lo:hi])
+                c_raw[a].append((lo, hi, part))
+
+        xq = [operand(S, f"xg{a}") for a in range(PASSES)]
+        cq = [operand(S, f"c{a}") for a in range(PASSES)]
+        uq = operand(PASSES * M, "u")
+
+        def multiply_x(a, j):
+            multiply(w4[:, a, :].bitcast(E2M1X4), w4_s[:, a * M : (a + 1) * M], xq[a], j, a == 0, False)
+
+        def multiply_c(a, j):
+            m = slice(a * M, (a + 1) * M)
+            multiply(uq[1][:, m].bitcast(E4M3X4), uq[2][:, m], cq[a], j, False, a == 1)
+
+        picked = keep.tile([P, PACK, S], F32, name="picked0")
+        for i in range(PACK):
+            gather(0, i, picked[:, i, :])
+        interleave(nc.scalar.copy, xq[0][0][:], picked[:])
+        quantize(xq[0][1][:], xq[0][2][:], xq[0][0][:])
+        for j in range(TILES):
+            multiply_x(0, j)
+
+        for a in range(PASSES):
+            interleave(nc.scalar.copy, uq[0][:, a * M : (a + 1) * M, :], u_raw[:, a, :].rearrange("p (i n) -> p i n", i=PACK))
+        quantize(uq[1][:], uq[2][:], uq[0][:])
+
+        for h in range(2):
+            pair = keep.tile([P, 2, S], F32, name=f"pair{h}")
+            for i in range(2):
+                gather(1, 2 * h + i, pair[:, i, :])
+            two = slice(2 * h, 2 * h + 2)
+            share(xq[1][0][:, :, two], pair[:], X_SCALAR[h])
+        quantize(xq[1][1][:], xq[1][2][:], xq[1][0][:])
+        for j in range(TILES):
+            multiply_x(1, j)
+
+        for a in range(PASSES):
+            for lo, hi, part in c_raw[a]:
+                share(cq[a][0][:, lo:hi, :], part[:], C_SCALAR[hi - lo])
+                for q_lo, q_hi in C_QUANTIZES[hi - lo]:
+                    cols = slice(lo + q_lo, lo + q_hi)
+                    quantize(cq[a][1][:, cols], cq[a][2][:, cols], cq[a][0][:, cols, :])
+                for j in range(lo // N_TILE, hi // N_TILE):
+                    multiply_c(a, j)
+                    if a == PASSES - 1:
+                        result = keep.tile([P, N_TILE], F32, name=f"result{j}")
+                        nc.scalar.activation(result[:], acc[j][:], SILU, bias=bias[:])
+                        nc.sync.dma_start(out[:, j * N_TILE : (j + 1) * N_TILE], result[:])

@@ -23,10 +23,9 @@ PASSES = 2
 N_TILE = 128
 TILES = S // N_TILE
 PIECE = 256
-X_SCALAR = [512, 192]
-C_LOADS = [[(0, S)], [(0, 384), (384, S)]]
-C_SCALAR = {512: 224, 384: 128, 128: 0}
-C_QUANTIZES = {512: [(0, 512)], 384: [(0, 128), (128, 384)], 128: [(0, 128)]}
+HALF = S // 2
+LAST = 384
+C_LOADS = [[(0, S)], [(0, LAST), (LAST, S)]]
 
 
 def tile_list_hmix_silu_kernel(tc, xT, w4_words, w4_scales, c, u, wgt, b, offs, out):
@@ -83,18 +82,12 @@ def tile_list_hmix_silu_kernel(tc, xT, w4_words, w4_scales, c, u, wgt, b, offs, 
                 rows.rearrange("p i (w v) -> p w i v", v=4),
             )
 
-        def share(grouped, rows, split):
-            width = rows.shape[2]
-            if split > 0:
-                interleave(nc.scalar.copy, grouped[:, 0:split, :], rows[:, :, 0:split])
-            if split < width:
-                interleave(nc.vector.tensor_copy, grouped[:, split:width, :], rows[:, :, split:width])
-
-        def quantize(codes, scales, grouped):
+        def quantize_cols(op, lo, hi):
+            grouped, codes, scales = op
             nc.vector.quantize_mx(
-                out=codes.bitcast(E4M3X4),
-                scales=scales,
-                in_=grouped.rearrange("p w i -> p (w i)"),
+                out=codes[:, lo:hi].bitcast(E4M3X4),
+                scales=scales[:, lo:hi],
+                in_=grouped[:, lo:hi, :].rearrange("p w i -> p (w i)"),
             )
 
         def operand(width, name):
@@ -128,7 +121,7 @@ def tile_list_hmix_silu_kernel(tc, xT, w4_words, w4_scales, c, u, wgt, b, offs, 
             for lo, hi in C_LOADS[a]:
                 part = keep.tile([P, PACK, hi - lo], F32, name=f"c_raw{a}_{lo}")
                 nc.sync.dma_start(part[:], c_src[a][:, :, lo:hi])
-                c_raw[a].append((lo, hi, part))
+                c_raw[a].append(part)
 
         xq = [operand(S, f"xg{a}") for a in range(PASSES)]
         cq = [operand(S, f"c{a}") for a in range(PASSES)]
@@ -145,33 +138,40 @@ def tile_list_hmix_silu_kernel(tc, xT, w4_words, w4_scales, c, u, wgt, b, offs, 
         for i in range(PACK):
             gather(0, i, picked[:, i, :])
         interleave(nc.scalar.copy, xq[0][0][:], picked[:])
-        quantize(xq[0][1][:], xq[0][2][:], xq[0][0][:])
-        for j in range(TILES):
-            multiply_x(0, j)
-
         for a in range(PASSES):
             interleave(nc.scalar.copy, uq[0][:, a * M : (a + 1) * M, :], u_raw[:, a, :].rearrange("p (i n) -> p i n", i=PACK))
-        quantize(uq[1][:], uq[2][:], uq[0][:])
 
-        for h in range(2):
-            pair = keep.tile([P, 2, S], F32, name=f"pair{h}")
-            for i in range(2):
-                gather(1, 2 * h + i, pair[:, i, :])
-            two = slice(2 * h, 2 * h + 2)
-            share(xq[1][0][:, :, two], pair[:], X_SCALAR[h])
-        quantize(xq[1][1][:], xq[1][2][:], xq[1][0][:])
+        pairs = [keep.tile([P, 2, S], F32, name=f"pair{h}") for h in range(2)]
+        gather(1, 0, pairs[0][:, 0, :])
+        quantize_cols(xq[0], 0, S)
+        for j in range(TILES):
+            multiply_x(0, j)
+        gather(1, 1, pairs[0][:, 1, :])
+        interleave(nc.scalar.copy, xq[1][0][:, :, 0:2], pairs[0][:])
+        quantize_cols(uq, 0, PASSES * M)
+        gather(1, 2, pairs[1][:, 0, :])
+        gather(1, 3, pairs[1][:, 1, :])
+        interleave(nc.vector.tensor_copy, xq[1][0][:, 0:HALF, 2:4], pairs[1][:, :, 0:HALF])
+        interleave(nc.scalar.copy, xq[1][0][:, HALF:S, 2:4], pairs[1][:, :, HALF:S])
+        quantize_cols(xq[1], 0, HALF)
+        quantize_cols(xq[1], HALF, S)
         for j in range(TILES):
             multiply_x(1, j)
 
-        for a in range(PASSES):
-            for lo, hi, part in c_raw[a]:
-                share(cq[a][0][:, lo:hi, :], part[:], C_SCALAR[hi - lo])
-                for q_lo, q_hi in C_QUANTIZES[hi - lo]:
-                    cols = slice(lo + q_lo, lo + q_hi)
-                    quantize(cq[a][1][:, cols], cq[a][2][:, cols], cq[a][0][:, cols, :])
-                for j in range(lo // N_TILE, hi // N_TILE):
-                    multiply_c(a, j)
-                    if a == PASSES - 1:
-                        result = keep.tile([P, N_TILE], F32, name=f"result{j}")
-                        nc.scalar.activation(result[:], acc[j][:], SILU, bias=bias[:])
-                        nc.sync.dma_start(out[:, j * N_TILE : (j + 1) * N_TILE], result[:])
+        interleave(nc.vector.tensor_copy, cq[0][0][:, 0:HALF, :], c_raw[0][0][:, :, 0:HALF])
+        interleave(nc.scalar.copy, cq[0][0][:, HALF:S, :], c_raw[0][0][:, :, HALF:S])
+        quantize_cols(cq[0], 0, HALF)
+        quantize_cols(cq[0], HALF, S)
+        for j in range(TILES):
+            multiply_c(0, j)
+        interleave(nc.vector.tensor_copy, cq[1][0][:, 0:HALF, :], c_raw[1][0][:, :, 0:HALF])
+        interleave(nc.scalar.copy, cq[1][0][:, HALF:LAST, :], c_raw[1][0][:, :, HALF:LAST])
+        interleave(nc.scalar.copy, cq[1][0][:, LAST:S, :], c_raw[1][1][:])
+        quantize_cols(cq[1], HALF, LAST)
+        quantize_cols(cq[1], 0, HALF)
+        quantize_cols(cq[1], LAST, S)
+        for j in (2, 0, 1, 3):
+            multiply_c(1, j)
+            result = keep.tile([P, N_TILE], F32, name=f"result{j}")
+            nc.scalar.activation(result[:], acc[j][:], SILU, bias=bias[:])
+            nc.sync.dma_start(out[:, j * N_TILE : (j + 1) * N_TILE], result[:])

@@ -1,6 +1,7 @@
 from contextlib import ExitStack
 
 import concourse.mybir as mybir
+from concourse.masks import make_identity
 
 K, L, M, T, S = 1024, 1024, 128, 2048, 512
 
@@ -44,14 +45,22 @@ def tile_list_hmix_silu_kernel(tc, xT, w4_words, w4_scales, c, u, wgt, b, offs, 
         weight = keep.tile([P, S], F32, name="weight")
         nc.sync.dma_start(weight[:], wgt)
 
-        bias = keep.tile([P, 1], F32, name="bias")
-        nc.scalar.dma_start(bias[:], b.rearrange("(p o) -> p o", o=1))
         scales_src = w4_scales.bitcast(I32).rearrange("a q n -> q a n")
         for q in range(4):
-            nc.scalar.dma_start(
+            nc.gpsimd.dma_start(
                 w4_s_words[32 * q : 32 * q + 4, :].rearrange("p (a n) -> p a n", a=PASSES),
                 scales_src[4 * q : 4 * q + 4, :, :],
             )
+
+        identity = keep.tile([P, P], F32, name="identity")
+        make_identity(nc, identity[:])
+        b_row = keep.tile([P, P], F32, name="b_row")
+        nc.vector.memset(b_row[:], 0.0)
+        nc.scalar.dma_start(b_row[0:1, :], b.rearrange("(o n) -> o n", o=1))
+        b_turned = psum.tile([P, P], F32, name="b_turned")
+        nc.tensor.transpose(b_turned[:], b_row[:], identity[:])
+        bias = keep.tile([P, 1], F32, name="bias")
+        nc.vector.tensor_copy(bias[:], b_turned[:, 0:1])
 
         warm = keep.tile([P, 1], F32, name="warm")
         warm_out = keep.tile([P, 1], F32, name="warm_out")
@@ -166,9 +175,10 @@ def tile_list_hmix_silu_kernel(tc, xT, w4_words, w4_scales, c, u, wgt, b, offs, 
             multiply_c(0, j)
         interleave(nc.vector.tensor_copy, cq[1][0][:, 0:HALF, :], c_raw[1][0][:, :, 0:HALF])
         interleave(nc.scalar.copy, cq[1][0][:, HALF:LAST, :], c_raw[1][0][:, :, HALF:LAST])
-        interleave(nc.scalar.copy, cq[1][0][:, LAST:S, :], c_raw[1][1][:])
         quantize_cols(cq[1], HALF, LAST)
         quantize_cols(cq[1], 0, HALF)
+        interleave(nc.scalar.copy, cq[1][0][:, LAST : LAST + 48, :], c_raw[1][1][:, :, 0:48])
+        interleave(nc.vector.tensor_copy, cq[1][0][:, LAST + 48 : S, :], c_raw[1][1][:, :, 48:128])
         quantize_cols(cq[1], LAST, S)
         for j in (2, 0, 1, 3):
             multiply_c(1, j)

@@ -25,8 +25,8 @@ N_TILE = 128
 TILES = S // N_TILE
 PIECE = 256
 HALF = S // 2
-LAST = 384
-C_LOADS = [[(0, S)], [(0, LAST), (LAST, S)]]
+C_LOADS = [[(0, S)], [(0, S)]]
+MEET = 320
 
 
 def tile_list_hmix_silu_kernel(tc, xT, w4_words, w4_scales, c, u, wgt, b, offs, out):
@@ -43,8 +43,15 @@ def tile_list_hmix_silu_kernel(tc, xT, w4_words, w4_scales, c, u, wgt, b, offs, 
         offsets = lists.tile([P, S // 16], U16, name="offsets")
         nc.sync.dma_start(offsets[:], offs)
         weight = keep.tile([P, S], F32, name="weight")
-        nc.sync.dma_start(weight[:], wgt)
+        nc.scalar.dma_start(weight[:], wgt)
 
+        w4 = keep.tile([P, PASSES, 2 * M], U8, name="w4", align_bytes=64)
+        nc.scalar.dma_start(
+            w4[:].rearrange("p a n -> p (a n)").bitcast(I32).rearrange("p (a n) -> p a n", a=PASSES),
+            w4_words.bitcast(I32).rearrange("a p n -> p a n"),
+        )
+        u_raw = keep.tile([P, PASSES, PACK * M], F32, name="u_raw")
+        nc.scalar.dma_start(u_raw[:], u.rearrange("(a p i) n -> p a (i n)", a=PASSES, i=PACK))
         scales_src = w4_scales.bitcast(I32).rearrange("a q n -> q a n")
         for q in range(4):
             nc.gpsimd.dma_start(
@@ -119,10 +126,6 @@ def tile_list_hmix_silu_kernel(tc, xT, w4_words, w4_scales, c, u, wgt, b, offs, 
 
         for i in range(PACK):
             load_x(0, i)
-        w4 = keep.tile([P, PASSES, 2 * M], U8, name="w4", align_bytes=64)
-        nc.sync.dma_start(w4[:], w4_words.rearrange("a p n -> p a n"))
-        u_raw = keep.tile([P, PASSES, PACK * M], F32, name="u_raw")
-        nc.sync.dma_start(u_raw[:], u.rearrange("(a p i) n -> p a (i n)", a=PASSES, i=PACK))
         for i in range(PACK):
             load_x(1, i)
         c_raw = [[], []]
@@ -173,15 +176,21 @@ def tile_list_hmix_silu_kernel(tc, xT, w4_words, w4_scales, c, u, wgt, b, offs, 
         quantize_cols(cq[0], HALF, S)
         for j in range(TILES):
             multiply_c(0, j)
-        interleave(nc.vector.tensor_copy, cq[1][0][:, 0:HALF, :], c_raw[1][0][:, :, 0:HALF])
-        interleave(nc.scalar.copy, cq[1][0][:, HALF:LAST, :], c_raw[1][0][:, :, HALF:LAST])
-        quantize_cols(cq[1], HALF, LAST)
-        quantize_cols(cq[1], 0, HALF)
-        interleave(nc.scalar.copy, cq[1][0][:, LAST : LAST + 48, :], c_raw[1][1][:, :, 0:48])
-        interleave(nc.vector.tensor_copy, cq[1][0][:, LAST + 48 : S, :], c_raw[1][1][:, :, 48:128])
-        quantize_cols(cq[1], LAST, S)
-        for j in (2, 0, 1, 3):
+        last = cq[1]
+        rows = c_raw[1][0]
+        for copy, lo, hi in (
+            (nc.vector.tensor_copy, 0, 128),
+            (nc.scalar.copy, 384, 512),
+            (nc.vector.tensor_copy, 128, 256),
+            (nc.scalar.copy, MEET, 384),
+            (nc.vector.tensor_copy, 256, MEET),
+        ):
+            interleave(copy, last[0][:, lo:hi, :], rows[:, :, lo:hi])
+        for j in (0, 1, 3, 2):
+            quantize_cols(last, j * N_TILE, (j + 1) * N_TILE)
+        for j in (0, 1, 3, 2):
             multiply_c(1, j)
             result = keep.tile([P, N_TILE], F32, name=f"result{j}")
             nc.scalar.activation(result[:], acc[j][:], SILU, bias=bias[:])
-            nc.sync.dma_start(out[:, j * N_TILE : (j + 1) * N_TILE], result[:])
+            queue = nc.scalar if j == 2 else nc.sync
+            queue.dma_start(out[:, j * N_TILE : (j + 1) * N_TILE], result[:])

from contextlib import ExitStack

import concourse.mybir as mybir
from concourse.masks import make_identity

K, L, M, T, S = 1024, 1024, 128, 2048, 512

F32 = mybir.dt.float32
BF16 = mybir.dt.bfloat16
I32 = mybir.dt.int32
U32 = mybir.dt.uint32
U16 = mybir.dt.uint16
U8 = mybir.dt.uint8
E4M3X4 = mybir.dt.float8_e4m3fn_x4
E2M1X4 = mybir.dt.float4_e2m1fn_x4
MULT = mybir.AluOpType.mult
SILU = mybir.ActivationFunctionType.Silu

FLOPS = 2 * M * S * (K + L)

P = 128
PACK = 4
PASSES = 2
N_TILE = 128
TILES = S // N_TILE
PIECE = 256
HALF = S // 2
C_LOADS = [[(0, S)], [(0, S)]]
MEET = 320


def tile_list_hmix_silu_kernel(tc, xT, w4_words, w4_scales, c, u, wgt, b, offs, out):
    nc = tc.nc
    with ExitStack() as ctx:
        lists = ctx.enter_context(tc.tile_pool(name="lists", bufs=1))
        keep = ctx.enter_context(tc.tile_pool(name="keep", bufs=1))
        psum = ctx.enter_context(tc.psum_pool(name="psum", bufs=1))

        w4_s = keep.tile([P, PASSES * M], U8, name="w4_s", align_bytes=64)
        w4_s_words = w4_s[:].bitcast(I32)
        nc.vector.memset(w4_s_words, 0)

        offsets = lists.tile([P, S // 16], U16, name="offsets")
        nc.sync.dma_start(offsets[:], offs)
        weight = keep.tile([P, S], F32, name="weight")
        nc.scalar.dma_start(weight[:], wgt)

        w4 = keep.tile([P, PASSES, 2 * M], U8, name="w4", align_bytes=64)
        nc.scalar.dma_start(
            w4[:].rearrange("p a n -> p (a n)").bitcast(I32).rearrange("p (a n) -> p a n", a=PASSES),
            w4_words.bitcast(I32).rearrange("a p n -> p a n"),
        )
        u_raw = keep.tile([P, PASSES, PACK * M], F32, name="u_raw")
        nc.scalar.dma_start(u_raw[:], u.rearrange("(a p i) n -> p a (i n)", a=PASSES, i=PACK))
        scales_src = w4_scales.bitcast(I32).rearrange("a q n -> q a n")
        for q in range(4):
            nc.gpsimd.dma_start(
                w4_s_words[32 * q : 32 * q + 4, :].rearrange("p (a n) -> p a n", a=PASSES),
                scales_src[4 * q : 4 * q + 4, :, :],
            )

        identity = keep.tile([P, P], F32, name="identity")
        make_identity(nc, identity[:])
        b_row = keep.tile([P, P], F32, name="b_row")
        nc.vector.memset(b_row[:], 0.0)
        nc.scalar.dma_start(b_row[0:1, :], b.rearrange("(o n) -> o n", o=1))
        b_turned = psum.tile([P, P], F32, name="b_turned")
        nc.tensor.transpose(b_turned[:], b_row[:], identity[:])
        bias = keep.tile([P, 1], F32, name="bias")
        nc.vector.tensor_copy(bias[:], b_turned[:, 0:1])

        warm = keep.tile([P, 1], F32, name="warm")
        warm_out = keep.tile([P, 1], F32, name="warm_out")
        nc.vector.memset(warm[:], 0.0)
        nc.scalar.activation(warm_out[:], warm[:], SILU)

        x_src = xT.rearrange("(a p i) t -> a i p t", a=PASSES, i=PACK)
        c_src = c.rearrange("(a p i) j -> a p i j", a=PASSES, i=PACK)
        acc = [psum.tile([P, N_TILE], F32, name=f"acc{j}") for j in range(TILES)]
        x_t = {}

        def load_x(a, i):
            x_t[a, i] = keep.tile([P, T], F32, name=f"x{a}{i}")
            nc.sync.dma_start(x_t[a, i][:], x_src[a, i])

        def gather(a, i, dst):
            for j in range(0, S, PIECE):
                nc.vector.tensor_tensor(
                    dst[:, j : j + PIECE],
                    x_t[a, i][:].indirect(offsets[:, j // 16 : (j + PIECE) // 16]),
                    weight[:, j : j + PIECE],
                    MULT,
                )

        def interleave(copy, grouped, rows):
            copy(
                grouped.rearrange("p (w v) i -> p w i v", v=4),
                rows.rearrange("p i (w v) -> p w i v", v=4),
            )

        def quantize_cols(op, lo, hi):
            grouped, codes, scales = op
            nc.vector.quantize_mx(
                out=codes[:, lo:hi].bitcast(E4M3X4),
                scales=scales[:, lo:hi],
                in_=grouped[:, lo:hi, :].rearrange("p w i -> p (w i)"),
            )

        def operand(width, name):
            grouped = keep.tile([P, width, PACK], BF16, name=name + "_grouped", align_bytes=64)
            codes = keep.tile([P, width], U32, name=name + "_codes", align_bytes=64)
            scales = keep.tile([P, width], U8, name=name + "_scales", align_bytes=64)
            return grouped, codes, scales

        def multiply(lhsT, lhsT_scale, rhs, j, start, stop):
            cols = slice(j * N_TILE, (j + 1) * N_TILE)
            nc.tensor.matmul_mx(
                out=acc[j][:],
                lhsT=lhsT,
                lhsT_scale=lhsT_scale,
                rhs=rhs[1][:, cols].bitcast(E4M3X4),
                rhs_scale=rhs[2][:, cols],
                start=start,
                stop=stop,
            )

        for i in range(PACK):
            load_x(0, i)
        for i in range(PACK):
            load_x(1, i)
        c_raw = [[], []]
        for a in range(PASSES):
            for lo, hi in C_LOADS[a]:
                part = keep.tile([P, PACK, hi - lo], F32, name=f"c_raw{a}_{lo}")
                nc.sync.dma_start(part[:], c_src[a][:, :, lo:hi])
                c_raw[a].append(part)

        xq = [operand(S, f"xg{a}") for a in range(PASSES)]
        cq = [operand(S, f"c{a}") for a in range(PASSES)]
        uq = operand(PASSES * M, "u")

        def multiply_x(a, j):
            multiply(w4[:, a, :].bitcast(E2M1X4), w4_s[:, a * M : (a + 1) * M], xq[a], j, a == 0, False)

        def multiply_c(a, j):
            m = slice(a * M, (a + 1) * M)
            multiply(uq[1][:, m].bitcast(E4M3X4), uq[2][:, m], cq[a], j, False, a == 1)

        picked = keep.tile([P, PACK, S], F32, name="picked0")
        for i in range(PACK):
            gather(0, i, picked[:, i, :])
        interleave(nc.scalar.copy, xq[0][0][:], picked[:])
        for a in range(PASSES):
            interleave(nc.scalar.copy, uq[0][:, a * M : (a + 1) * M, :], u_raw[:, a, :].rearrange("p (i n) -> p i n", i=PACK))

        pairs = [keep.tile([P, 2, S], F32, name=f"pair{h}") for h in range(2)]
        gather(1, 0, pairs[0][:, 0, :])
        quantize_cols(xq[0], 0, S)
        for j in range(TILES):
            multiply_x(0, j)
        gather(1, 1, pairs[0][:, 1, :])
        interleave(nc.scalar.copy, xq[1][0][:, :, 0:2], pairs[0][:])
        quantize_cols(uq, 0, PASSES * M)
        gather(1, 2, pairs[1][:, 0, :])
        gather(1, 3, pairs[1][:, 1, :])
        interleave(nc.vector.tensor_copy, xq[1][0][:, 0:HALF, 2:4], pairs[1][:, :, 0:HALF])
        interleave(nc.scalar.copy, xq[1][0][:, HALF:S, 2:4], pairs[1][:, :, HALF:S])
        quantize_cols(xq[1], 0, HALF)
        quantize_cols(xq[1], HALF, S)
        for j in range(TILES):
            multiply_x(1, j)

        interleave(nc.vector.tensor_copy, cq[0][0][:, 0:HALF, :], c_raw[0][0][:, :, 0:HALF])
        interleave(nc.scalar.copy, cq[0][0][:, HALF:S, :], c_raw[0][0][:, :, HALF:S])
        quantize_cols(cq[0], 0, HALF)
        quantize_cols(cq[0], HALF, S)
        for j in range(TILES):
            multiply_c(0, j)
        last = cq[1]
        rows = c_raw[1][0]
        for copy, lo, hi in (
            (nc.vector.tensor_copy, 0, 128),
            (nc.scalar.copy, 384, 512),
            (nc.vector.tensor_copy, 128, 256),
            (nc.scalar.copy, MEET, 384),
            (nc.vector.tensor_copy, 256, MEET),
        ):
            interleave(copy, last[0][:, lo:hi, :], rows[:, :, lo:hi])
        for j in (0, 1, 3, 2):
            quantize_cols(last, j * N_TILE, (j + 1) * N_TILE)
        for j in (0, 1, 3, 2):
            multiply_c(1, j)
            result = keep.tile([P, N_TILE], F32, name=f"result{j}")
            nc.scalar.activation(result[:], acc[j][:], SILU, bias=bias[:])
            queue = nc.scalar if j == 2 else nc.sync
            queue.dma_start(out[:, j * N_TILE : (j + 1) * N_TILE], result[:])
